import numpy as np
import ml_dtypes


def mxq(x, axis, fmt="e4m3"):
    dtype, down = {"e4m3": (ml_dtypes.float8_e4m3fn, 7), "e5m2": (ml_dtypes.float8_e5m2, 14)}[fmt]
    v = np.moveaxis(np.asarray(x, np.float32).astype(ml_dtypes.bfloat16).astype(np.float64), axis, -1)
    blocks = v.reshape(v.shape[:-1] + (-1, 32))
    amax = np.abs(blocks).max(-1, keepdims=True)
    byte = np.maximum(np.where(amax > 0, np.frexp(amax)[1] - 1 + 127, 0) - down, 1)
    scale = np.exp2(byte - 127.0)
    codes = (blocks / scale).astype(np.float32).astype(dtype).astype(np.float64)
    return np.moveaxis((codes * scale).reshape(v.shape), -1, axis)


WIDE = False


def mx_kscale(k):
    if not WIDE:
        return np.ones(k)
    levels = np.array([10, -10, 5, -5, 0])
    if k % 512:
        return np.exp2(np.random.permutation(np.resize(levels, k // 32))).repeat(32)
    a = np.empty((k // 512, 16))
    for p in range(k // 512):
        a[p, :8] = np.random.permutation(np.resize(levels, 8))
        for g in range(8):
            far = levels[np.abs(levels - a[p, g]) >= 10]
            a[p, g + 8] = far[np.random.randint(len(far))]
    return np.exp2(a.ravel()).repeat(32)


def f64(x):
    return np.asarray(x).astype(np.float64)


def striped(idx):
    return np.tile(idx.reshape(-1, 16).T, (8, 1)).astype(np.uint16)


def unstriped(offs):
    return offs[:16].T.reshape(-1).astype(np.int64)


E2M1 = np.array([0.0, 0.5, 1.0, 1.5, 2.0, 3.0, 4.0, 6.0, -0.0, -0.5, -1.0, -1.5, -2.0, -3.0, -4.0, -6.0])


def pack_weight(w, fmt):
    k, n = w.shape
    w = f64(np.asarray(w, np.float32).astype(ml_dtypes.bfloat16)).reshape(k // 32, 32, n)
    amax = np.abs(w).max(1)
    if fmt == "e4m3":
        byte = np.frexp(amax)[1] - 1 + 127 - 7
    else:
        mant, ex = np.frexp(amax / 6.0)
        byte = np.where(mant > 0.5, ex, ex - 1) + 127
    byte = np.clip(np.where(amax > 0, byte, 1), 1, 254)
    scaled = (w * np.exp2(127.0 - byte)[:, None, :]).reshape(k, n).astype(np.float32)
    by_word = np.ascontiguousarray(scaled.reshape(k // 512, 128, 4, n).transpose(0, 1, 3, 2))
    if fmt == "e4m3":
        words = by_word.astype(ml_dtypes.float8_e4m3fn).view(np.uint8)
    else:
        c = by_word.astype(ml_dtypes.float4_e2m1fn).view(np.uint8) & 0xF
        words = (c[..., 0::2] | (c[..., 1::2] << 4)).reshape(k // 512, 128, 2 * n)
    return np.ascontiguousarray(words), np.ascontiguousarray(byte.astype(np.uint8).reshape(k // 512, 16, n))


def unpack_weight(words, scales, fmt):
    g, _, n = scales.shape
    words = np.ascontiguousarray(words).reshape(g, 128, n, -1)
    if fmt == "e4m3":
        vals = words.view(ml_dtypes.float8_e4m3fn).astype(np.float64)
    else:
        nib = np.empty((g, 128, n, 4), np.uint8)
        nib[..., 0::2] = words & 0xF
        nib[..., 1::2] = words >> 4
        vals = E2M1[nib]
    vals = vals * np.repeat(np.exp2(scales.astype(np.float64) - 127.0), 8, axis=1)[..., None]
    return vals.transpose(0, 1, 3, 2).reshape(g * 512, n)


def sigmoid(v):
    return 1.0 / (1.0 + np.exp(-np.maximum(v, -700.0)))


K, T, E, C, H, N = 1024, 512, 8, 256, 512, 128
TOP = 4


def by_expert(wq, xq):
    return np.concatenate([wq[e].T @ xq[:, e * C:(e + 1) * C] for e in range(E)], axis=1)


def setup_inputs():
    n = np.random.standard_normal
    s = mx_kscale(K)[:, None]
    u = mx_kscale(H)
    deal = np.repeat(np.arange(E), C).reshape(TOP, T)[:, np.random.permutation(T)]
    deal = np.take_along_axis(deal, np.argsort(np.random.rand(TOP, T), axis=0), axis=0)
    for _ in range(8):
        s_, t_ = np.random.permutation(T).reshape(2, -1); r = np.random.randint(TOP, size=T // 2); x, y = deal[r, s_].copy(), deal[r, t_].copy()
        ok = ~((deal[:, s_] == y).any(0) | (deal[:, t_] == x).any(0)); deal[r[ok], s_[ok]] = y[ok]; deal[r[ok], t_[ok]] = x[ok]
    order = np.lexsort((np.random.rand(TOP * T), deal.reshape(-1)))
    slot_token = order % T; pos = np.empty(TOP * T, np.int64); pos[order] = np.arange(TOP * T); pos = pos.reshape(TOP, T)
    g = np.random.uniform(0.5, 1.5, (TOP, T)); g = g / g.sum(0)
    w1 = [pack_weight(m, "e2m1") for m in n((E, K, H)) / np.sqrt(K) / s[None]]
    w3 = [pack_weight(m, "e2m1") for m in n((E, K, H)) / np.sqrt(K) / s[None] * u[None, None, :]]
    w2 = [pack_weight(m, "e2m1") for m in n((E, H, N)) / np.sqrt(H) / u[None, :, None]]
    return {
        "xT": (n((K, T)) * s).astype(np.float32),
        "w1_words": np.stack([m[0] for m in w1]),
        "w1_scales": np.stack([m[1] for m in w1]),
        "w3_words": np.stack([m[0] for m in w3]),
        "w3_scales": np.stack([m[1] for m in w3]),
        "w2_words": np.stack([m[0] for m in w2]),
        "w2_scales": np.stack([m[1] for m in w2]),
        "gate": np.stack([np.tile(r, (N, 1)) for r in g]).astype(np.float32),
        "offs": striped(slot_token),
        "pos1": striped(pos[0]),
        "pos2": striped(pos[1]),
        "pos3": striped(pos[2]),
        "pos4": striped(pos[3]),
    }


def reference(xT, w1_words, w1_scales, w3_words, w3_scales, w2_words, w2_scales, gate, offs, pos1, pos2, pos3, pos4):
    idx = unstriped(offs)
    w1 = np.stack([unpack_weight(w1_words[e], w1_scales[e], "e2m1") for e in range(E)])
    w3 = np.stack([unpack_weight(w3_words[e], w3_scales[e], "e2m1") for e in range(E)])
    w2 = np.stack([unpack_weight(w2_words[e], w2_scales[e], "e2m1") for e in range(E)])
    xq = mxq(f64(xT)[:, idx], 0, "e4m3")
    h = sigmoid(by_expert(w1, xq))
    h = h * by_expert(w3, xq)
    y = by_expert(w2, mxq(h, 0, "e4m3"))
    return sum(f64(gate[r]) * y[:, unstriped(p)] for r, p in enumerate((pos1, pos2, pos3, pos4)))

@@ -1,0 +1,262 @@
+from contextlib import ExitStack
+
+import concourse.mybir as mybir
+from concourse.masks import make_identity
+
+F32 = mybir.dt.float32
+BF16 = mybir.dt.bfloat16
+I32 = mybir.dt.int32
+U32 = mybir.dt.uint32
+U16 = mybir.dt.uint16
+U8 = mybir.dt.uint8
+FP8X4 = mybir.dt.float8_e4m3fn_x4
+FP4X4 = mybir.dt.float4_e2m1fn_x4
+COPY = mybir.ActivationFunctionType.Copy
+SIGMOID = mybir.ActivationFunctionType.Sigmoid
+MULT = mybir.AluOpType.mult
+ADD = mybir.AluOpType.add
+
+P = 128
+K, T, E, C, H, N, TOP = 1024, 512, 8, 256, 512, 128, 4
+SLOTS = E * C
+PASSES = K // 512
+FLOPS = 2 * SLOTS * (2 * K * H + H * N)
+
+PIECES = (256, 384, 384, 384, 384, 256)
+SHIFTS = (256, 384, 768, 640)
+GPSIMD_TILES = (0,)
+RING = 3
+
+
+def tile_moe_tk_glu_sigmoid_kernel(
+    tc, xT, w1_words, w1_scales, w3_words, w3_scales, w2_words, w2_scales, gate, offs, pos1, pos2, pos3, pos4, out
+):
+    nc = tc.nc
+    with ExitStack() as ctx:
+        lists = ctx.enter_context(tc.tile_pool(name="lists", bufs=1))
+        keep = ctx.enter_context(tc.tile_pool(name="keep", bufs=1))
+        ring = ctx.enter_context(tc.tile_pool(name="ring", bufs=RING))
+        work = ctx.enter_context(tc.tile_pool(name="work", bufs=4))
+        psum = ctx.enter_context(tc.psum_pool(name="psum", bufs=3))
+        psum_2 = ctx.enter_context(tc.psum_pool(name="psum_2", bufs=1))
+
+        offs_t = lists.tile([P, SLOTS // 16], U16, name="offs_t")
+        pos_t = [lists.tile([P, T // 16], U16, name=f"pos{r}_t") for r in range(TOP)]
+
+        x_raw = [keep.tile([P, 4, T], F32, name=f"x_raw{s}", align_bytes=64) for s in range(PASSES)]
+        x_bf = [keep.tile([P, T, 4], BF16, name=f"x_bf{s}", align_bytes=64) for s in range(PASSES)]
+        x_codes = [keep.tile([P, T], U32, name=f"x_codes{s}", align_bytes=64) for s in range(PASSES)]
+        x_bytes = keep.tile([P, T], U8, name="x_bytes", align_bytes=64)
+        s_codes = [keep.tile([P, SLOTS], U32, name=f"s_codes{s}", align_bytes=64) for s in range(PASSES)]
+        s_bytes = [keep.tile([P, SLOTS], U8, name=f"s_bytes{s}", align_bytes=64) for s in range(PASSES)]
+        w2_t = keep.tile([P, E, 2 * N], U8, name="w2_t", align_bytes=64)
+        w1_s = keep.tile([P, E, PASSES, H], U8, name="w1_s", align_bytes=64)
+        w3_s = keep.tile([P, E, PASSES, H], U8, name="w3_s", align_bytes=64)
+        w2_s = keep.tile([P, E, N], U8, name="w2_s", align_bytes=64)
+        y_t = keep.tile([P, SLOTS], F32, name="y_t", align_bytes=64)
+        out_t = keep.tile([P, T], F32, name="out_t", align_bytes=64)
+        ident = keep.tile([P, P], F32, name="ident", align_bytes=64)
+        warm = keep.tile([P, 2], F32, name="warm", align_bytes=64)
+
+        half = T // 2
+        nc.sync.dma_start(x_raw[0][:], xT[0:512, :].rearrange("(p j) w -> p j w", j=4))
+        nc.sync.dma_start(offs_t[:], offs)
+        nc.sync.dma_start(x_raw[1][:], xT[512:1024, :].rearrange("(p j) w -> p j w", j=4))
+
+        nc.vector.memset(warm[:], 0.0)
+        nc.scalar.activation(warm[:, 0:1], warm[:, 1:2], SIGMOID)
+        for t in (w1_s, w3_s):
+            nc.gpsimd.memset(t[:, 0:4].bitcast(I32), 0)
+            nc.vector.memset(t[:, 4:E].bitcast(I32), 0)
+        nc.gpsimd.memset(x_bytes[:], 0)
+        nc.gpsimd.memset(s_bytes[1][:].bitcast(I32), 0)
+        nc.gpsimd.memset(w2_s[:].bitcast(I32), 0)
+        make_identity(nc, ident[:])
+
+        def load_scales(e0, e1):
+            for t, src in ((w1_s, w1_scales), (w3_s, w3_scales)):
+                view = src.bitcast(I32).rearrange("e s q i -> q (e s) i")
+                for quad in range(4):
+                    nc.sync.dma_start(
+                        t[32 * quad : 32 * quad + 4, e0:e1].bitcast(I32).rearrange("q e s i -> q (e s) i"),
+                        view[4 * quad : 4 * quad + 4, e0 * PASSES : e1 * PASSES, :],
+                    )
+
+        w_tiles = {}
+        gates = {}
+
+        def load_ring(i):
+            if i < E:
+                w = ring.tile([P, 2, PASSES, 2 * H], U8, name="w", align_bytes=64)
+                for m, src in enumerate((w1_words, w3_words)):
+                    nc.sync.dma_start(w[:, m].bitcast(I32), src.bitcast(I32)[i].rearrange("s p c -> p s c"))
+                w_tiles[i] = w
+            elif i < E + 2:
+                r = 2 * (i - E)
+                g = ring.tile([P, 2, T], F32, name="w", align_bytes=64)
+                nc.sync.dma_start(g[:], gate[r : r + 2].rearrange("r p t -> p r t"))
+                gates[r] = g[:, 0]
+                gates[r + 1] = g[:, 1]
+
+        load_scales(0, E)
+        load_ring(0)
+        load_ring(1)
+        nc.sync.dma_start(w2_t[:].bitcast(I32), w2_words.bitcast(I32).rearrange("e s p c -> p (e s) c"))
+        for quad in range(4):
+            nc.sync.dma_start(
+                w2_s[32 * quad : 32 * quad + 4].bitcast(I32),
+                w2_scales.bitcast(I32).rearrange("e s q i -> q (e s) i")[4 * quad : 4 * quad + 4],
+            )
+        for i in range(2, RING):
+            load_ring(i)
+
+        starts = [sum(PIECES[:i]) for i in range(len(PIECES))]
+
+        def cast(s, a, b, engine_copy):
+            engine_copy(x_bf[s][:, a:b, :], x_raw[s][:, :, a:b].rearrange("p j w -> p w j"))
+
+        def quantize_tokens(s):
+            nc.vector.quantize_mx(
+                out=x_codes[s][:].bitcast(FP8X4),
+                scales=x_bytes[4 * s : P, :],
+                in_=x_bf[s][:].rearrange("p w j -> p (w j)"),
+            )
+
+        def gather_codes(s, i):
+            a, n = starts[i], PIECES[i]
+            nc.vector.tensor_copy(s_codes[s][:, a : a + n], x_codes[s][:].indirect(offs_t[:, a // 16 : (a + n) // 16]))
+
+        def gather_bytes(i):
+            a, n = starts[i], PIECES[i]
+            nc.vector.tensor_copy(s_bytes[0][:, a : a + n], x_bytes[:].indirect(offs_t[:, a // 16 : (a + n) // 16]))
+
+        def shift_bytes(i):
+            a = sum(SHIFTS[:i])
+            b = a + SHIFTS[i]
+            nc.sync.dma_start(s_bytes[1][0 : P - 4, a:b].bitcast(I32), s_bytes[0][4:P, a:b].bitcast(I32))
+
+        cast(0, 320, 512, nc.scalar.copy)
+        cast(0, 0, 320, nc.vector.tensor_copy)
+        quantize_tokens(0)
+        gather_codes(0, 0)
+        cast(1, 208, 512, nc.scalar.copy)
+        cast(1, 0, 208, nc.vector.tensor_copy)
+        quantize_tokens(1)
+        gather_bytes(0)
+        shift_bytes(0)
+        gather_codes(1, 0)
+        gather_bytes(1)
+        shift_bytes(1)
+        gather_codes(0, 1)
+        gather_codes(1, 1)
+        gather_bytes(2)
+        gather_bytes(3)
+        shift_bytes(2)
+        gather_codes(0, 2)
+        gather_codes(1, 2)
+
+        after = {
+            0: lambda: (gather_bytes(4), gather_bytes(5), shift_bytes(3)),
+            1: lambda: (gather_codes(0, 3), gather_codes(1, 3)),
+            2: lambda: (gather_codes(0, 4), gather_codes(1, 4)),
+            3: lambda: (gather_codes(0, 5), gather_codes(1, 5)),
+        }
+        h_tiles = {}
+
+        def multiply_1(e, st):
+            slots = slice(e * C + st * P, e * C + (st + 1) * P)
+            banks = []
+            for m, (name, scales) in enumerate((("bank_a", w1_s), ("bank_b", w3_s))):
+                bank = psum.tile([P, H], F32, name=name)
+                for s in range(PASSES):
+                    nc.tensor.matmul_mx(
+                        out=bank[:],
+                        lhsT=s_codes[s][:, slots].bitcast(FP8X4),
+                        lhsT_scale=s_bytes[s][:, slots],
+                        rhs=w_tiles[e][:, m, s, :].bitcast(FP4X4),
+                        rhs_scale=scales[:, e, s, :],
+                        start=(s == 0),
+                        stop=(s == PASSES - 1),
+                    )
+                banks.append(bank)
+            return banks
+
+        def activate(e, st, banks):
+            sig = work.tile([P, H], F32, name="sig")
+            nc.scalar.activation(sig[:], banks[0][:], SIGMOID)
+            h = work.tile([P, H], BF16, name="h", align_bytes=64)
+            if st in GPSIMD_TILES:
+                lin = work.tile([P, H], F32, name="lin")
+                nc.scalar.copy(lin[:], banks[1][:])
+                nc.gpsimd.tensor_tensor(h[:], lin[:], sig[:], MULT)
+            else:
+                nc.vector.tensor_tensor(h[:], banks[1][:], sig[:], MULT)
+            h_tiles[e, st] = h
+
+        def turn(e, tiles):
+            n = len(tiles) * P
+            turned = psum_2.tile([P, 2, n], F32, name="turned")
+            for x, st in enumerate(tiles):
+                words = h_tiles[e, st][:].bitcast(F32)
+                for u in range(2):
+                    nc.tensor.transpose(turned[:, u, x * P : (x + 1) * P], words[:, u::2], ident[:])
+            h_bf = work.tile([P, 4 * n], BF16, name="h_bf", align_bytes=64)
+            nc.scalar.copy(h_bf[:].bitcast(F32).rearrange("p (r u) -> p r u", u=2), turned[:].rearrange("p u r -> p r u"))
+            return h_bf
+
+        def quantize_hidden(h_bf):
+            n = h_bf.shape[1] // 4
+            h_codes = work.tile([P, n], U32, name="h_codes", align_bytes=64)
+            h_bytes = work.tile([P, n], U8, name="h_bytes", align_bytes=64)
+            nc.vector.quantize_mx(out=h_codes[:].bitcast(FP8X4), scales=h_bytes[:], in_=h_bf[:])
+            return h_codes, h_bytes
+
+        def multiply_2(e, a, h_codes, h_bytes):
+            n = h_codes.shape[1]
+            bank = psum_2.tile([P, n], F32, name="bank_y")
+            nc.tensor.matmul_mx(
+                out=bank[:],
+                lhsT=w2_t[:, e, :].bitcast(FP4X4),
+                lhsT_scale=w2_s[:, e, :],
+                rhs=h_codes[:].bitcast(FP8X4),
+                rhs_scale=h_bytes[:],
+                start=True,
+                stop=True,
+            )
+            nc.scalar.copy(y_t[:, a : a + n], bank[:])
+
+        quantized = {}
+        for e in range(E):
+            activate(e, 0, multiply_1(e, 0))
+            activate(e, 1, multiply_1(e, 1))
+            if e >= 2:
+                multiply_2(e - 2, (e - 2) * C, *quantized[e - 2])
+            if e >= 1:
+                h_bf = turn(e - 1, (0, 1))
+            if e >= 1:
+                quantized[e - 1] = quantize_hidden(h_bf)
+            load_ring(e + RING)
+            if e in after:
+                after[e]()
+            if e == 3:
+                for r, src in enumerate((pos1, pos2, pos3, pos4)):
+                    nc.sync.dma_start(pos_t[r][:], src)
+        last = E - 1
+        h_first = turn(last, (0,))
+        multiply_2(last - 1, (last - 1) * C, *quantized[last - 1])
+        first = quantize_hidden(h_first)
+        h_second = turn(last, (1,))
+        multiply_2(last, last * C, *first)
+        multiply_2(last, last * C + P, *quantize_hidden(h_second))
+
+        for hf in range(2):
+            cols = slice(hf * half, (hf + 1) * half)
+            parts = work.tile([P, TOP, half], F32, name="parts")
+            for r in range(TOP):
+                nc.vector.tensor_tensor(
+                    parts[:, r], y_t[:].indirect(pos_t[r][:, hf * half // 16 : (hf + 1) * half // 16]), gates[r][:, cols], MULT
+                )
+            pairs = work.tile([P, 2, half], F32, name="pairs")
+            nc.vector.tensor_tensor(pairs[:], parts[:, 0:2], parts[:, 2:4], ADD)
+            nc.vector.tensor_tensor(out_t[:, cols], pairs[:, 0], pairs[:, 1], ADD)
+            nc.sync.dma_start(out[:, cols], out_t[:, cols])

@@ -11,7 +11,6 @@ U16 = mybir.dt.uint16
 U8 = mybir.dt.uint8
 FP8X4 = mybir.dt.float8_e4m3fn_x4
 FP4X4 = mybir.dt.float4_e2m1fn_x4
-COPY = mybir.ActivationFunctionType.Copy
 SIGMOID = mybir.ActivationFunctionType.Sigmoid
 MULT = mybir.AluOpType.mult
 ADD = mybir.AluOpType.add
@@ -22,10 +21,9 @@ SLOTS = E * C
 PASSES = K // 512
 FLOPS = 2 * SLOTS * (2 * K * H + H * N)
 
-PIECES = (256, 384, 384, 384, 384, 256)
-SHIFTS = (256, 384, 768, 640)
-GPSIMD_TILES = (0,)
 RING = 3
+EARLY = 3
+GPSIMD_EXPERTS = (2, 3, 4, 5, 6)
 
 
 def tile_moe_tk_glu_sigmoid_kernel(
@@ -45,42 +43,34 @@ def tile_moe_tk_glu_sigmoid_kernel(
 
         x_raw = [keep.tile([P, 4, T], F32, name=f"x_raw{s}", align_bytes=64) for s in range(PASSES)]
         x_bf = [keep.tile([P, T, 4], BF16, name=f"x_bf{s}", align_bytes=64) for s in range(PASSES)]
+        shifted = keep.tile([P, RING, C], U8, name="shifted", align_bytes=64)
         x_codes = [keep.tile([P, T], U32, name=f"x_codes{s}", align_bytes=64) for s in range(PASSES)]
         x_bytes = keep.tile([P, T], U8, name="x_bytes", align_bytes=64)
-        s_codes = [keep.tile([P, SLOTS], U32, name=f"s_codes{s}", align_bytes=64) for s in range(PASSES)]
-        s_bytes = [keep.tile([P, SLOTS], U8, name=f"s_bytes{s}", align_bytes=64) for s in range(PASSES)]
-        w2_t = keep.tile([P, E, 2 * N], U8, name="w2_t", align_bytes=64)
-        w1_s = keep.tile([P, E, PASSES, H], U8, name="w1_s", align_bytes=64)
-        w3_s = keep.tile([P, E, PASSES, H], U8, name="w3_s", align_bytes=64)
-        w2_s = keep.tile([P, E, N], U8, name="w2_s", align_bytes=64)
+        early_scales = [keep.tile([P, EARLY, PASSES, H], U8, name=f"early_scales{m}", align_bytes=64) for m in range(2)]
         y_t = keep.tile([P, SLOTS], F32, name="y_t", align_bytes=64)
         out_t = keep.tile([P, T], F32, name="out_t", align_bytes=64)
         ident = keep.tile([P, P], F32, name="ident", align_bytes=64)
         warm = keep.tile([P, 2], F32, name="warm", align_bytes=64)
 
-        half = T // 2
         nc.sync.dma_start(x_raw[0][:], xT[0:512, :].rearrange("(p j) w -> p j w", j=4))
         nc.sync.dma_start(offs_t[:], offs)
         nc.sync.dma_start(x_raw[1][:], xT[512:1024, :].rearrange("(p j) w -> p j w", j=4))
 
         nc.vector.memset(warm[:], 0.0)
         nc.scalar.activation(warm[:, 0:1], warm[:, 1:2], SIGMOID)
-        for t in (w1_s, w3_s):
-            nc.gpsimd.memset(t[:, 0:4].bitcast(I32), 0)
-            nc.vector.memset(t[:, 4:E].bitcast(I32), 0)
+        for t in early_scales:
+            nc.vector.memset(t[:].bitcast(I32), 0)
         nc.gpsimd.memset(x_bytes[:], 0)
-        nc.gpsimd.memset(s_bytes[1][:].bitcast(I32), 0)
-        nc.gpsimd.memset(w2_s[:].bitcast(I32), 0)
+        nc.gpsimd.memset(shifted[:].bitcast(I32), 0)
         make_identity(nc, ident[:])
 
-        def load_scales(e0, e1):
-            for t, src in ((w1_s, w1_scales), (w3_s, w3_scales)):
-                view = src.bitcast(I32).rearrange("e s q i -> q (e s) i")
-                for quad in range(4):
-                    nc.sync.dma_start(
-                        t[32 * quad : 32 * quad + 4, e0:e1].bitcast(I32).rearrange("q e s i -> q (e s) i"),
-                        view[4 * quad : 4 * quad + 4, e0 * PASSES : e1 * PASSES, :],
-                    )
+        def load_scales(t, src, e0, e1, queue):
+            view = src.bitcast(I32).rearrange("e s q i -> q (e s) i")
+            for quad in range(4):
+                queue.dma_start(
+                    t[32 * quad : 32 * quad + 4].bitcast(I32).rearrange("q e s i -> q (e s) i"),
+                    view[4 * quad : 4 * quad + 4, e0 * PASSES : e1 * PASSES, :],
+                )
 
         w_tiles = {}
         gates = {}
@@ -98,19 +88,11 @@ def tile_moe_tk_glu_sigmoid_kernel(
                 gates[r] = g[:, 0]
                 gates[r + 1] = g[:, 1]
 
-        load_scales(0, E)
+        for t, src in zip(early_scales, (w1_scales, w3_scales)):
+            load_scales(t, src, 0, EARLY, nc.sync)
         load_ring(0)
         load_ring(1)
-        nc.sync.dma_start(w2_t[:].bitcast(I32), w2_words.bitcast(I32).rearrange("e s p c -> p (e s) c"))
-        for quad in range(4):
-            nc.sync.dma_start(
-                w2_s[32 * quad : 32 * quad + 4].bitcast(I32),
-                w2_scales.bitcast(I32).rearrange("e s q i -> q (e s) i")[4 * quad : 4 * quad + 4],
-            )
-        for i in range(2, RING):
-            load_ring(i)
-
-        starts = [sum(PIECES[:i]) for i in range(len(PIECES))]
+        load_ring(2)
 
         def cast(s, a, b, engine_copy):
             engine_copy(x_bf[s][:, a:b, :], x_raw[s][:, :, a:b].rearrange("p j w -> p w j"))
@@ -122,18 +104,23 @@ def tile_moe_tk_glu_sigmoid_kernel(
                 in_=x_bf[s][:].rearrange("p w j -> p (w j)"),
             )
 
-        def gather_codes(s, i):
-            a, n = starts[i], PIECES[i]
-            nc.vector.tensor_copy(s_codes[s][:, a : a + n], x_codes[s][:].indirect(offs_t[:, a // 16 : (a + n) // 16]))
+        s_codes = {}
+        s_bytes = {}
 
-        def gather_bytes(i):
-            a, n = starts[i], PIECES[i]
-            nc.vector.tensor_copy(s_bytes[0][:, a : a + n], x_bytes[:].indirect(offs_t[:, a // 16 : (a + n) // 16]))
+        def expert_offsets(e):
+            return offs_t[:, e * C // 16 : (e + 1) * C // 16]
 
-        def shift_bytes(i):
-            a = sum(SHIFTS[:i])
-            b = a + SHIFTS[i]
-            nc.sync.dma_start(s_bytes[1][0 : P - 4, a:b].bitcast(I32), s_bytes[0][4:P, a:b].bitcast(I32))
+        def gather_codes(s, e):
+            codes = ring.tile([P, C], U32, name=f"s_codes{s}", align_bytes=64)
+            nc.vector.tensor_copy(codes[:], x_codes[s][:].indirect(expert_offsets(e)))
+            s_codes[s, e] = codes
+
+        def gather_bytes(e, queue):
+            both = ring.tile([P, C], U8, name="s_bytes0", align_bytes=64)
+            nc.vector.tensor_copy(both[:], x_bytes[:].indirect(expert_offsets(e)))
+            queue.dma_start(shifted[0 : P - 4, e % RING].bitcast(I32), both[4:P, :].bitcast(I32))
+            s_bytes[0, e] = both
+            s_bytes[1, e] = shifted[:, e % RING]
 
         cast(0, 320, 512, nc.scalar.copy)
         cast(0, 0, 320, nc.vector.tensor_copy)
@@ -142,39 +129,45 @@ def tile_moe_tk_glu_sigmoid_kernel(
         cast(1, 208, 512, nc.scalar.copy)
         cast(1, 0, 208, nc.vector.tensor_copy)
         quantize_tokens(1)
-        gather_bytes(0)
-        shift_bytes(0)
+        gather_bytes(0, nc.scalar)
         gather_codes(1, 0)
-        gather_bytes(1)
-        shift_bytes(1)
-        gather_codes(0, 1)
-        gather_codes(1, 1)
-        gather_bytes(2)
-        gather_bytes(3)
-        shift_bytes(2)
-        gather_codes(0, 2)
-        gather_codes(1, 2)
+        for e in range(1, RING):
+            gather_bytes(e, nc.sync)
+            gather_codes(0, e)
+            gather_codes(1, e)
 
-        after = {
-            0: lambda: (gather_bytes(4), gather_bytes(5), shift_bytes(3)),
-            1: lambda: (gather_codes(0, 3), gather_codes(1, 3)),
-            2: lambda: (gather_codes(0, 4), gather_codes(1, 4)),
-            3: lambda: (gather_codes(0, 5), gather_codes(1, 5)),
-        }
+        late_scales = []
+        for m, src in enumerate((w1_scales, w3_scales)):
+            t = keep.tile([P, E - EARLY, PASSES, H], U8, name=f"x_raw{m}", align_bytes=64)
+            nc.gpsimd.memset(t[:].bitcast(I32), 0)
+            load_scales(t, src, EARLY, E, nc.gpsimd)
+            late_scales.append(t)
+        w2_all = keep.tile([P, E, 3 * N], U8, name="x_bf1", align_bytes=64)
+        w2_t = w2_all[:].rearrange("p e c -> p (e c)")[:, 0 : E * 2 * N].rearrange("p (e c) -> p e c", e=E)
+        w2_s = w2_all[:].rearrange("p e c -> p (e c)")[:, E * 2 * N :].rearrange("p (e c) -> p e c", e=E)
+        nc.gpsimd.memset(w2_s.bitcast(I32), 0)
+        nc.sync.dma_start(w2_t.bitcast(I32), w2_words.bitcast(I32).rearrange("e s p c -> p (e s) c"))
+        for quad in range(4):
+            nc.sync.dma_start(
+                w2_s[32 * quad : 32 * quad + 4].bitcast(I32),
+                w2_scales.bitcast(I32).rearrange("e s q i -> q (e s) i")[4 * quad : 4 * quad + 4],
+            )
+
         h_tiles = {}
 
         def multiply_1(e, st):
-            slots = slice(e * C + st * P, e * C + (st + 1) * P)
+            slots = slice(st * P, (st + 1) * P)
             banks = []
-            for m, (name, scales) in enumerate((("bank_a", w1_s), ("bank_b", w3_s))):
+            for m, name in enumerate(("bank_a", "bank_b")):
+                scales = early_scales[m][:, e] if e < EARLY else late_scales[m][:, e - EARLY]
                 bank = psum.tile([P, H], F32, name=name)
                 for s in range(PASSES):
                     nc.tensor.matmul_mx(
                         out=bank[:],
-                        lhsT=s_codes[s][:, slots].bitcast(FP8X4),
-                        lhsT_scale=s_bytes[s][:, slots],
+                        lhsT=s_codes[s, e][:, slots].bitcast(FP8X4),
+                        lhsT_scale=s_bytes[s, e][:, slots],
                         rhs=w_tiles[e][:, m, s, :].bitcast(FP4X4),
-                        rhs_scale=scales[:, e, s, :],
+                        rhs_scale=scales[:, s, :],
                         start=(s == 0),
                         stop=(s == PASSES - 1),
                     )
@@ -185,7 +178,7 @@ def tile_moe_tk_glu_sigmoid_kernel(
             sig = work.tile([P, H], F32, name="sig")
             nc.scalar.activation(sig[:], banks[0][:], SIGMOID)
             h = work.tile([P, H], BF16, name="h", align_bytes=64)
-            if st in GPSIMD_TILES:
+            if st == 0 and e in GPSIMD_EXPERTS:
                 lin = work.tile([P, H], F32, name="lin")
                 nc.scalar.copy(lin[:], banks[1][:])
                 nc.gpsimd.tensor_tensor(h[:], lin[:], sig[:], MULT)
@@ -193,7 +186,7 @@ def tile_moe_tk_glu_sigmoid_kernel(
                 nc.vector.tensor_tensor(h[:], banks[1][:], sig[:], MULT)
             h_tiles[e, st] = h
 
-        def turn(e, tiles):
+        def turn(e, tiles, engine_copy):
             n = len(tiles) * P
             turned = psum_2.tile([P, 2, n], F32, name="turned")
             for x, st in enumerate(tiles):
@@ -201,7 +194,7 @@ def tile_moe_tk_glu_sigmoid_kernel(
                 for u in range(2):
                     nc.tensor.transpose(turned[:, u, x * P : (x + 1) * P], words[:, u::2], ident[:])
             h_bf = work.tile([P, 4 * n], BF16, name="h_bf", align_bytes=64)
-            nc.scalar.copy(h_bf[:].bitcast(F32).rearrange("p (r u) -> p r u", u=2), turned[:].rearrange("p u r -> p r u"))
+            engine_copy(h_bf[:].bitcast(F32).rearrange("p (r u) -> p r u", u=2), turned[:].rearrange("p u r -> p r u"))
             return h_bf
 
         def quantize_hidden(h_bf):
@@ -211,11 +204,9 @@ def tile_moe_tk_glu_sigmoid_kernel(
             nc.vector.quantize_mx(out=h_codes[:].bitcast(FP8X4), scales=h_bytes[:], in_=h_bf[:])
             return h_codes, h_bytes
 
-        def multiply_2(e, a, h_codes, h_bytes):
-            n = h_codes.shape[1]
-            bank = psum_2.tile([P, n], F32, name="bank_y")
+        def multiply_2(e, target, h_codes, h_bytes):
             nc.tensor.matmul_mx(
-                out=bank[:],
+                out=target,
                 lhsT=w2_t[:, e, :].bitcast(FP4X4),
                 lhsT_scale=w2_s[:, e, :],
                 rhs=h_codes[:].bitcast(FP8X4),
@@ -223,40 +214,55 @@ def tile_moe_tk_glu_sigmoid_kernel(
                 start=True,
                 stop=True,
             )
-            nc.scalar.copy(y_t[:, a : a + n], bank[:])
 
         quantized = {}
+        y_banks = {}
+
+        def second_layer(e):
+            if e % 2 == 0:
+                y_bank = psum_2.tile([P, 2 * C], F32, name="y_bank")
+                y_banks[e] = y_bank
+                multiply_2(e, y_bank[:, 0:C], *quantized[e])
+            else:
+                y_bank = y_banks[e - 1]
+                multiply_2(e, y_bank[:, C : 2 * C], *quantized[e])
+                nc.scalar.copy(y_t[:, (e - 1) * C : (e + 1) * C], y_bank[:])
+
+        last = E - 1
         for e in range(E):
             activate(e, 0, multiply_1(e, 0))
             activate(e, 1, multiply_1(e, 1))
             if e >= 2:
-                multiply_2(e - 2, (e - 2) * C, *quantized[e - 2])
+                second_layer(e - 2)
             if e >= 1:
-                h_bf = turn(e - 1, (0, 1))
-            if e >= 1:
+                h_bf = turn(e - 1, (0, 1), nc.scalar.copy)
                 quantized[e - 1] = quantize_hidden(h_bf)
             load_ring(e + RING)
-            if e in after:
-                after[e]()
+            if e + RING < E:
+                gather_bytes(e + RING, nc.sync)
+                gather_codes(0, e + RING)
+                gather_codes(1, e + RING)
             if e == 3:
                 for r, src in enumerate((pos1, pos2, pos3, pos4)):
                     nc.sync.dma_start(pos_t[r][:], src)
-        last = E - 1
-        h_first = turn(last, (0,))
-        multiply_2(last - 1, (last - 1) * C, *quantized[last - 1])
-        first = quantize_hidden(h_first)
-        h_second = turn(last, (1,))
-        multiply_2(last, last * C, *first)
-        multiply_2(last, last * C + P, *quantize_hidden(h_second))
 
+        first = quantize_hidden(turn(last, (0,), nc.scalar.copy))
+        second_layer(last - 1)
+        y_bank = y_banks[last - 1]
+        multiply_2(last, y_bank[:, C : C + P], *first)
+        nc.scalar.copy(y_t[:, (last - 1) * C : last * C + P], y_bank[:, 0 : C + P])
+        second = quantize_hidden(turn(last, (1,), nc.vector.tensor_copy))
+        y_last = psum.tile([P, P], F32, name="bank_a")
+        multiply_2(last, y_last[:], *second)
+        nc.vector.tensor_copy(y_t[:, last * C + P :], y_last[:])
+
+        parts = keep.tile([P, TOP, T], F32, name="parts", align_bytes=64)
+        for r in range(TOP):
+            nc.vector.tensor_tensor(parts[:, r], y_t[:].indirect(pos_t[r][:]), gates[r], MULT)
+        pairs = keep.tile([P, 2, T], F32, name="pairs", align_bytes=64)
+        nc.vector.tensor_tensor(pairs[:], parts[:, 0:2], parts[:, 2:4], ADD)
+        half = T // 2
         for hf in range(2):
             cols = slice(hf * half, (hf + 1) * half)
-            parts = work.tile([P, TOP, half], F32, name="parts")
-            for r in range(TOP):
-                nc.vector.tensor_tensor(
-                    parts[:, r], y_t[:].indirect(pos_t[r][:, hf * half // 16 : (hf + 1) * half // 16]), gates[r][:, cols], MULT
-                )
-            pairs = work.tile([P, 2, half], F32, name="pairs")
-            nc.vector.tensor_tensor(pairs[:], parts[:, 0:2], parts[:, 2:4], ADD)
-            nc.vector.tensor_tensor(out_t[:, cols], pairs[:, 0], pairs[:, 1], ADD)
+            nc.vector.tensor_tensor(out_t[:, cols], pairs[:, 0, cols], pairs[:, 1, cols], ADD)
             nc.sync.dma_start(out[:, cols], out_t[:, cols])

@@ -23,7 +23,10 @@ FLOPS = 2 * SLOTS * (2 * K * H + H * N)
 
 RING = 3
 EARLY = 3
-GPSIMD_EXPERTS = (2, 3, 4, 5, 6)
+GPSIMD_EXPERTS = (2, 3, 4, 5)
+PIECES = ((0,), (1, 2), (3, 4), (5, 6), (7,))
+AHEAD = 3
+WINDOW = 2 * T
 
 
 def tile_moe_tk_glu_sigmoid_kernel(
@@ -34,6 +37,7 @@ def tile_moe_tk_glu_sigmoid_kernel(
         lists = ctx.enter_context(tc.tile_pool(name="lists", bufs=1))
         keep = ctx.enter_context(tc.tile_pool(name="keep", bufs=1))
         ring = ctx.enter_context(tc.tile_pool(name="ring", bufs=RING))
+        gathered = ctx.enter_context(tc.tile_pool(name="gathered", bufs=AHEAD))
         work = ctx.enter_context(tc.tile_pool(name="work", bufs=4))
         psum = ctx.enter_context(tc.psum_pool(name="psum", bufs=3))
         psum_2 = ctx.enter_context(tc.psum_pool(name="psum_2", bufs=1))
@@ -43,9 +47,9 @@ def tile_moe_tk_glu_sigmoid_kernel(
 
         x_raw = [keep.tile([P, 4, T], F32, name=f"x_raw{s}", align_bytes=64) for s in range(PASSES)]
         x_bf = [keep.tile([P, T, 4], BF16, name=f"x_bf{s}", align_bytes=64) for s in range(PASSES)]
-        shifted = keep.tile([P, RING, C], U8, name="shifted", align_bytes=64)
-        x_codes = [keep.tile([P, T], U32, name=f"x_codes{s}", align_bytes=64) for s in range(PASSES)]
-        x_bytes = keep.tile([P, T], U8, name="x_bytes", align_bytes=64)
+        shifted = keep.tile([P, AHEAD, 2 * C], U8, name="shifted", align_bytes=64)
+        x_codes = [keep.tile([P, WINDOW], U32, name=f"x_codes{s}", align_bytes=64) for s in range(PASSES)]
+        x_bytes = keep.tile([P, WINDOW], U8, name="x_bytes", align_bytes=64)
         early_scales = [keep.tile([P, EARLY, PASSES, H], U8, name=f"early_scales{m}", align_bytes=64) for m in range(2)]
         y_t = keep.tile([P, SLOTS], F32, name="y_t", align_bytes=64)
         out_t = keep.tile([P, T], F32, name="out_t", align_bytes=64)
@@ -60,6 +64,8 @@ def tile_moe_tk_glu_sigmoid_kernel(
         nc.scalar.activation(warm[:, 0:1], warm[:, 1:2], SIGMOID)
         for t in early_scales:
             nc.vector.memset(t[:].bitcast(I32), 0)
+        for t in x_codes:
+            nc.vector.memset(t[:, T:WINDOW].bitcast(I32), 0)
         nc.gpsimd.memset(x_bytes[:], 0)
         nc.gpsimd.memset(shifted[:].bitcast(I32), 0)
         make_identity(nc, ident[:])
@@ -99,28 +105,33 @@ def tile_moe_tk_glu_sigmoid_kernel(
 
         def quantize_tokens(s):
             nc.vector.quantize_mx(
-                out=x_codes[s][:].bitcast(FP8X4),
-                scales=x_bytes[4 * s : P, :],
+                out=x_codes[s][:, 0:T].bitcast(FP8X4),
+                scales=x_bytes[4 * s : P, 0:T],
                 in_=x_bf[s][:].rearrange("p w j -> p (w j)"),
             )
 
         s_codes = {}
         s_bytes = {}
 
-        def expert_offsets(e):
-            return offs_t[:, e * C // 16 : (e + 1) * C // 16]
+        def gather_bytes(i, queue):
+            experts = PIECES[i]
+            n = len(experts) * C
+            a = experts[0] * C
+            both = gathered.tile([P, n], U8, name="s_bytes", align_bytes=64)
+            nc.vector.tensor_copy(both[:], x_bytes[:].indirect(offs_t[:, a // 16 : (a + n) // 16]))
+            queue.dma_start(shifted[0 : P - 4, i % AHEAD, 0:n].bitcast(I32), both[4:P, :].bitcast(I32))
+            for x, e in enumerate(experts):
+                s_bytes[0, e] = both[:, x * C : (x + 1) * C]
+                s_bytes[1, e] = shifted[:, i % AHEAD, x * C : (x + 1) * C]
 
-        def gather_codes(s, e):
-            codes = ring.tile([P, C], U32, name=f"s_codes{s}", align_bytes=64)
-            nc.vector.tensor_copy(codes[:], x_codes[s][:].indirect(expert_offsets(e)))
-            s_codes[s, e] = codes
-
-        def gather_bytes(e, queue):
-            both = ring.tile([P, C], U8, name="s_bytes0", align_bytes=64)
-            nc.vector.tensor_copy(both[:], x_bytes[:].indirect(expert_offsets(e)))
-            queue.dma_start(shifted[0 : P - 4, e % RING].bitcast(I32), both[4:P, :].bitcast(I32))
-            s_bytes[0, e] = both
-            s_bytes[1, e] = shifted[:, e % RING]
+        def gather_codes(s, i):
+            experts = PIECES[i]
+            n = len(experts) * C
+            a = experts[0] * C
+            codes = gathered.tile([P, n], U32, name=f"s_codes{s}", align_bytes=64)
+            nc.vector.tensor_copy(codes[:], x_codes[s][:].indirect(offs_t[:, a // 16 : (a + n) // 16]))
+            for x, e in enumerate(experts):
+                s_codes[s, e] = codes[:, x * C : (x + 1) * C]
 
         cast(0, 320, 512, nc.scalar.copy)
         cast(0, 0, 320, nc.vector.tensor_copy)
@@ -131,10 +142,10 @@ def tile_moe_tk_glu_sigmoid_kernel(
         quantize_tokens(1)
         gather_bytes(0, nc.scalar)
         gather_codes(1, 0)
-        for e in range(1, RING):
-            gather_bytes(e, nc.sync)
-            gather_codes(0, e)
-            gather_codes(1, e)
+        for i in range(1, AHEAD):
+            gather_bytes(i, nc.scalar if i == 1 else nc.sync)
+            gather_codes(0, i)
+            gather_codes(1, i)
 
         late_scales = []
         for m, src in enumerate((w1_scales, w3_scales)):
@@ -238,10 +249,10 @@ def tile_moe_tk_glu_sigmoid_kernel(
                 h_bf = turn(e - 1, (0, 1), nc.scalar.copy)
                 quantized[e - 1] = quantize_hidden(h_bf)
             load_ring(e + RING)
-            if e + RING < E:
-                gather_bytes(e + RING, nc.sync)
-                gather_codes(0, e + RING)
-                gather_codes(1, e + RING)
+            if e % 2 == 0 and e // 2 + AHEAD < len(PIECES):
+                gather_bytes(e // 2 + AHEAD, nc.sync)
+                gather_codes(0, e // 2 + AHEAD)
+                gather_codes(1, e // 2 + AHEAD)
             if e == 3:
                 for r, src in enumerate((pos1, pos2, pos3, pos4)):
                     nc.sync.dma_start(pos_t[r][:], src)

@@ -23,7 +23,6 @@ FLOPS = 2 * SLOTS * (2 * K * H + H * N)
 
 RING = 3
 EARLY = 3
-GPSIMD_EXPERTS = (2, 3, 4, 5)
 PIECES = ((0,), (1, 2), (3, 4), (5, 6), (7,))
 AHEAD = 3
 WINDOW = 2 * T
@@ -38,6 +37,7 @@ def tile_moe_tk_glu_sigmoid_kernel(
         keep = ctx.enter_context(tc.tile_pool(name="keep", bufs=1))
         ring = ctx.enter_context(tc.tile_pool(name="ring", bufs=RING))
         gathered = ctx.enter_context(tc.tile_pool(name="gathered", bufs=AHEAD))
+        gathered_0 = ctx.enter_context(tc.tile_pool(name="gathered_0", bufs=AHEAD - 1))
         work = ctx.enter_context(tc.tile_pool(name="work", bufs=4))
         psum = ctx.enter_context(tc.psum_pool(name="psum", bufs=3))
         psum_2 = ctx.enter_context(tc.psum_pool(name="psum_2", bufs=1))
@@ -128,7 +128,7 @@ def tile_moe_tk_glu_sigmoid_kernel(
             experts = PIECES[i]
             n = len(experts) * C
             a = experts[0] * C
-            codes = gathered.tile([P, n], U32, name=f"s_codes{s}", align_bytes=64)
+            codes = (gathered_0 if s == 0 else gathered).tile([P, n], U32, name=f"s_codes{s}", align_bytes=64)
             nc.vector.tensor_copy(codes[:], x_codes[s][:].indirect(offs_t[:, a // 16 : (a + n) // 16]))
             for x, e in enumerate(experts):
                 s_codes[s, e] = codes[:, x * C : (x + 1) * C]
@@ -144,7 +144,8 @@ def tile_moe_tk_glu_sigmoid_kernel(
         gather_codes(1, 0)
         for i in range(1, AHEAD):
             gather_bytes(i, nc.scalar if i == 1 else nc.sync)
-            gather_codes(0, i)
+            if i < AHEAD - 1:
+                gather_codes(0, i)
             gather_codes(1, i)
 
         late_scales = []
@@ -189,12 +190,7 @@ def tile_moe_tk_glu_sigmoid_kernel(
             sig = work.tile([P, H], F32, name="sig")
             nc.scalar.activation(sig[:], banks[0][:], SIGMOID)
             h = work.tile([P, H], BF16, name="h", align_bytes=64)
-            if st == 0 and e in GPSIMD_EXPERTS:
-                lin = work.tile([P, H], F32, name="lin")
-                nc.scalar.copy(lin[:], banks[1][:])
-                nc.gpsimd.tensor_tensor(h[:], lin[:], sig[:], MULT)
-            else:
-                nc.vector.tensor_tensor(h[:], banks[1][:], sig[:], MULT)
+            nc.vector.tensor_tensor(h[:], banks[1][:], sig[:], MULT)
             h_tiles[e, st] = h
 
         def turn(e, tiles, engine_copy):
@@ -249,10 +245,13 @@ def tile_moe_tk_glu_sigmoid_kernel(
                 h_bf = turn(e - 1, (0, 1), nc.scalar.copy)
                 quantized[e - 1] = quantize_hidden(h_bf)
             load_ring(e + RING)
-            if e % 2 == 0 and e // 2 + AHEAD < len(PIECES):
-                gather_bytes(e // 2 + AHEAD, nc.sync)
-                gather_codes(0, e // 2 + AHEAD)
-                gather_codes(1, e // 2 + AHEAD)
+            if e % 2 == 0:
+                i = e // 2 + AHEAD
+                if i - 1 < len(PIECES):
+                    gather_codes(0, i - 1)
+                if i < len(PIECES):
+                    gather_bytes(i, nc.sync)
+                    gather_codes(1, i)
             if e == 3:
                 for r, src in enumerate((pos1, pos2, pos3, pos4)):
                     nc.sync.dma_start(pos_t[r][:], src)

from contextlib import ExitStack

import concourse.mybir as mybir
from concourse.masks import make_identity

F32 = mybir.dt.float32
BF16 = mybir.dt.bfloat16
I32 = mybir.dt.int32
U32 = mybir.dt.uint32
U16 = mybir.dt.uint16
U8 = mybir.dt.uint8
FP8X4 = mybir.dt.float8_e4m3fn_x4
FP4X4 = mybir.dt.float4_e2m1fn_x4
SIGMOID = mybir.ActivationFunctionType.Sigmoid
MULT = mybir.AluOpType.mult
ADD = mybir.AluOpType.add

P = 128
K, T, E, C, H, N, TOP = 1024, 512, 8, 256, 512, 128, 4
SLOTS = E * C
PASSES = K // 512
FLOPS = 2 * SLOTS * (2 * K * H + H * N)

RING = 3
EARLY = 3
PIECES = ((0,), (1, 2), (3, 4), (5, 6), (7,))
AHEAD = 3
WINDOW = 2 * T


def tile_moe_tk_glu_sigmoid_kernel(
    tc, xT, w1_words, w1_scales, w3_words, w3_scales, w2_words, w2_scales, gate, offs, pos1, pos2, pos3, pos4, out
):
    nc = tc.nc
    with ExitStack() as ctx:
        lists = ctx.enter_context(tc.tile_pool(name="lists", bufs=1))
        keep = ctx.enter_context(tc.tile_pool(name="keep", bufs=1))
        ring = ctx.enter_context(tc.tile_pool(name="ring", bufs=RING))
        gathered = ctx.enter_context(tc.tile_pool(name="gathered", bufs=AHEAD))
        gathered_0 = ctx.enter_context(tc.tile_pool(name="gathered_0", bufs=AHEAD - 1))
        work = ctx.enter_context(tc.tile_pool(name="work", bufs=4))
        psum = ctx.enter_context(tc.psum_pool(name="psum", bufs=3))
        psum_2 = ctx.enter_context(tc.psum_pool(name="psum_2", bufs=1))

        offs_t = lists.tile([P, SLOTS // 16], U16, name="offs_t")
        pos_t = [lists.tile([P, T // 16], U16, name=f"pos{r}_t") for r in range(TOP)]

        x_raw = [keep.tile([P, 4, T], F32, name=f"x_raw{s}", align_bytes=64) for s in range(PASSES)]
        x_bf = [keep.tile([P, T, 4], BF16, name=f"x_bf{s}", align_bytes=64) for s in range(PASSES)]
        shifted = keep.tile([P, AHEAD, 2 * C], U8, name="shifted", align_bytes=64)
        x_codes = [keep.tile([P, WINDOW], U32, name=f"x_codes{s}", align_bytes=64) for s in range(PASSES)]
        x_bytes = keep.tile([P, WINDOW], U8, name="x_bytes", align_bytes=64)
        early_scales = [keep.tile([P, EARLY, PASSES, H], U8, name=f"early_scales{m}", align_bytes=64) for m in range(2)]
        y_t = keep.tile([P, SLOTS], F32, name="y_t", align_bytes=64)
        out_t = keep.tile([P, T], F32, name="out_t", align_bytes=64)
        ident = keep.tile([P, P], F32, name="ident", align_bytes=64)
        warm = keep.tile([P, 2], F32, name="warm", align_bytes=64)

        nc.sync.dma_start(x_raw[0][:], xT[0:512, :].rearrange("(p j) w -> p j w", j=4))
        nc.sync.dma_start(offs_t[:], offs)
        nc.sync.dma_start(x_raw[1][:], xT[512:1024, :].rearrange("(p j) w -> p j w", j=4))

        nc.vector.memset(warm[:], 0.0)
        nc.scalar.activation(warm[:, 0:1], warm[:, 1:2], SIGMOID)
        for t in early_scales:
            nc.vector.memset(t[:].bitcast(I32), 0)
        for t in x_codes:
            nc.vector.memset(t[:, T:WINDOW].bitcast(I32), 0)
        nc.gpsimd.memset(x_bytes[:], 0)
        nc.gpsimd.memset(shifted[:].bitcast(I32), 0)
        make_identity(nc, ident[:])

        def load_scales(t, src, e0, e1, queue):
            view = src.bitcast(I32).rearrange("e s q i -> q (e s) i")
            for quad in range(4):
                queue.dma_start(
                    t[32 * quad : 32 * quad + 4].bitcast(I32).rearrange("q e s i -> q (e s) i"),
                    view[4 * quad : 4 * quad + 4, e0 * PASSES : e1 * PASSES, :],
                )

        w_tiles = {}
        gates = {}

        def load_ring(i):
            if i < E:
                w = ring.tile([P, 2, PASSES, 2 * H], U8, name="w", align_bytes=64)
                for m, src in enumerate((w1_words, w3_words)):
                    nc.sync.dma_start(w[:, m].bitcast(I32), src.bitcast(I32)[i].rearrange("s p c -> p s c"))
                w_tiles[i] = w
            elif i < E + 2:
                r = 2 * (i - E)
                g = ring.tile([P, 2, T], F32, name="w", align_bytes=64)
                nc.sync.dma_start(g[:], gate[r : r + 2].rearrange("r p t -> p r t"))
                gates[r] = g[:, 0]
                gates[r + 1] = g[:, 1]

        for t, src in zip(early_scales, (w1_scales, w3_scales)):
            load_scales(t, src, 0, EARLY, nc.sync)
        load_ring(0)
        load_ring(1)
        load_ring(2)

        def cast(s, a, b, engine_copy):
            engine_copy(x_bf[s][:, a:b, :], x_raw[s][:, :, a:b].rearrange("p j w -> p w j"))

        def quantize_tokens(s):
            nc.vector.quantize_mx(
                out=x_codes[s][:, 0:T].bitcast(FP8X4),
                scales=x_bytes[4 * s : P, 0:T],
                in_=x_bf[s][:].rearrange("p w j -> p (w j)"),
            )

        s_codes = {}
        s_bytes = {}

        def gather_bytes(i, queue):
            experts = PIECES[i]
            n = len(experts) * C
            a = experts[0] * C
            both = gathered.tile([P, n], U8, name="s_bytes", align_bytes=64)
            nc.vector.tensor_copy(both[:], x_bytes[:].indirect(offs_t[:, a // 16 : (a + n) // 16]))
            queue.dma_start(shifted[0 : P - 4, i % AHEAD, 0:n].bitcast(I32), both[4:P, :].bitcast(I32))
            for x, e in enumerate(experts):
                s_bytes[0, e] = both[:, x * C : (x + 1) * C]
                s_bytes[1, e] = shifted[:, i % AHEAD, x * C : (x + 1) * C]

        def gather_codes(s, i):
            experts = PIECES[i]
            n = len(experts) * C
            a = experts[0] * C
            codes = (gathered_0 if s == 0 else gathered).tile([P, n], U32, name=f"s_codes{s}", align_bytes=64)
            nc.vector.tensor_copy(codes[:], x_codes[s][:].indirect(offs_t[:, a // 16 : (a + n) // 16]))
            for x, e in enumerate(experts):
                s_codes[s, e] = codes[:, x * C : (x + 1) * C]

        cast(0, 320, 512, nc.scalar.copy)
        cast(0, 0, 320, nc.vector.tensor_copy)
        quantize_tokens(0)
        gather_codes(0, 0)
        cast(1, 208, 512, nc.scalar.copy)
        cast(1, 0, 208, nc.vector.tensor_copy)
        quantize_tokens(1)
        gather_bytes(0, nc.scalar)
        gather_codes(1, 0)
        for i in range(1, AHEAD):
            gather_bytes(i, nc.scalar if i == 1 else nc.sync)
            if i < AHEAD - 1:
                gather_codes(0, i)
            gather_codes(1, i)

        late_scales = []
        for m, src in enumerate((w1_scales, w3_scales)):
            t = keep.tile([P, E - EARLY, PASSES, H], U8, name=f"x_raw{m}", align_bytes=64)
            nc.gpsimd.memset(t[:].bitcast(I32), 0)
            load_scales(t, src, EARLY, E, nc.gpsimd)
            late_scales.append(t)
        w2_all = keep.tile([P, E, 3 * N], U8, name="x_bf1", align_bytes=64)
        w2_t = w2_all[:].rearrange("p e c -> p (e c)")[:, 0 : E * 2 * N].rearrange("p (e c) -> p e c", e=E)
        w2_s = w2_all[:].rearrange("p e c -> p (e c)")[:, E * 2 * N :].rearrange("p (e c) -> p e c", e=E)
        nc.gpsimd.memset(w2_s.bitcast(I32), 0)
        nc.sync.dma_start(w2_t.bitcast(I32), w2_words.bitcast(I32).rearrange("e s p c -> p (e s) c"))
        for quad in range(4):
            nc.sync.dma_start(
                w2_s[32 * quad : 32 * quad + 4].bitcast(I32),
                w2_scales.bitcast(I32).rearrange("e s q i -> q (e s) i")[4 * quad : 4 * quad + 4],
            )

        h_tiles = {}

        def multiply_1(e, st):
            slots = slice(st * P, (st + 1) * P)
            banks = []
            for m, name in enumerate(("bank_a", "bank_b")):
                scales = early_scales[m][:, e] if e < EARLY else late_scales[m][:, e - EARLY]
                bank = psum.tile([P, H], F32, name=name)
                for s in range(PASSES):
                    nc.tensor.matmul_mx(
                        out=bank[:],
                        lhsT=s_codes[s, e][:, slots].bitcast(FP8X4),
                        lhsT_scale=s_bytes[s, e][:, slots],
                        rhs=w_tiles[e][:, m, s, :].bitcast(FP4X4),
                        rhs_scale=scales[:, s, :],
                        start=(s == 0),
                        stop=(s == PASSES - 1),
                    )
                banks.append(bank)
            return banks

        def activate(e, st, banks):
            sig = work.tile([P, H], F32, name="sig")
            nc.scalar.activation(sig[:], banks[0][:], SIGMOID)
            h = work.tile([P, H], BF16, name="h", align_bytes=64)
            nc.vector.tensor_tensor(h[:], banks[1][:], sig[:], MULT)
            h_tiles[e, st] = h

        def turn(e, tiles, engine_copy):
            n = len(tiles) * P
            turned = psum_2.tile([P, 2, n], F32, name="turned")
            for x, st in enumerate(tiles):
                words = h_tiles[e, st][:].bitcast(F32)
                for u in range(2):
                    nc.tensor.transpose(turned[:, u, x * P : (x + 1) * P], words[:, u::2], ident[:])
            h_bf = work.tile([P, 4 * n], BF16, name="h_bf", align_bytes=64)
            engine_copy(h_bf[:].bitcast(F32).rearrange("p (r u) -> p r u", u=2), turned[:].rearrange("p u r -> p r u"))
            return h_bf

        def quantize_hidden(h_bf):
            n = h_bf.shape[1] // 4
            h_codes = work.tile([P, n], U32, name="h_codes", align_bytes=64)
            h_bytes = work.tile([P, n], U8, name="h_bytes", align_bytes=64)
            nc.vector.quantize_mx(out=h_codes[:].bitcast(FP8X4), scales=h_bytes[:], in_=h_bf[:])
            return h_codes, h_bytes

        def multiply_2(e, target, h_codes, h_bytes):
            nc.tensor.matmul_mx(
                out=target,
                lhsT=w2_t[:, e, :].bitcast(FP4X4),
                lhsT_scale=w2_s[:, e, :],
                rhs=h_codes[:].bitcast(FP8X4),
                rhs_scale=h_bytes[:],
                start=True,
                stop=True,
            )

        quantized = {}
        y_banks = {}

        def second_layer(e):
            if e % 2 == 0:
                y_bank = psum_2.tile([P, 2 * C], F32, name="y_bank")
                y_banks[e] = y_bank
                multiply_2(e, y_bank[:, 0:C], *quantized[e])
            else:
                y_bank = y_banks[e - 1]
                multiply_2(e, y_bank[:, C : 2 * C], *quantized[e])
                nc.scalar.copy(y_t[:, (e - 1) * C : (e + 1) * C], y_bank[:])

        last = E - 1
        for e in range(E):
            activate(e, 0, multiply_1(e, 0))
            activate(e, 1, multiply_1(e, 1))
            if e >= 2:
                second_layer(e - 2)
            if e >= 1:
                h_bf = turn(e - 1, (0, 1), nc.scalar.copy)
                quantized[e - 1] = quantize_hidden(h_bf)
            load_ring(e + RING)
            if e % 2 == 0:
                i = e // 2 + AHEAD
                if i - 1 < len(PIECES):
                    gather_codes(0, i - 1)
                if i < len(PIECES):
                    gather_bytes(i, nc.sync)
                    gather_codes(1, i)
            if e == 3:
                for r, src in enumerate((pos1, pos2, pos3, pos4)):
                    nc.sync.dma_start(pos_t[r][:], src)

        first = quantize_hidden(turn(last, (0,), nc.scalar.copy))
        second_layer(last - 1)
        y_bank = y_banks[last - 1]
        multiply_2(last, y_bank[:, C : C + P], *first)
        nc.scalar.copy(y_t[:, (last - 1) * C : last * C + P], y_bank[:, 0 : C + P])
        second = quantize_hidden(turn(last, (1,), nc.vector.tensor_copy))
        y_last = psum.tile([P, P], F32, name="bank_a")
        multiply_2(last, y_last[:], *second)
        nc.vector.tensor_copy(y_t[:, last * C + P :], y_last[:])

        parts = keep.tile([P, TOP, T], F32, name="parts", align_bytes=64)
        for r in range(TOP):
            nc.vector.tensor_tensor(parts[:, r], y_t[:].indirect(pos_t[r][:]), gates[r], MULT)
        pairs = keep.tile([P, 2, T], F32, name="pairs", align_bytes=64)
        nc.vector.tensor_tensor(pairs[:], parts[:, 0:2], parts[:, 2:4], ADD)
        half = T // 2
        for hf in range(2):
            cols = slice(hf * half, (hf + 1) * half)
            nc.vector.tensor_tensor(out_t[:, cols], pairs[:, 0, cols], pairs[:, 1, cols], ADD)
            nc.sync.dma_start(out[:, cols], out_t[:, cols])
